import numpy as np
import ml_dtypes


def mxq(x, axis, fmt="e4m3"):
    dtype, down = {"e4m3": (ml_dtypes.float8_e4m3fn, 7), "e5m2": (ml_dtypes.float8_e5m2, 14)}[fmt]
    v = np.moveaxis(np.asarray(x, np.float32).astype(ml_dtypes.bfloat16).astype(np.float64), axis, -1)
    blocks = v.reshape(v.shape[:-1] + (-1, 32))
    amax = np.abs(blocks).max(-1, keepdims=True)
    byte = np.maximum(np.where(amax > 0, np.frexp(amax)[1] - 1 + 127, 0) - down, 1)
    scale = np.exp2(byte - 127.0)
    codes = (blocks / scale).astype(np.float32).astype(dtype).astype(np.float64)
    return np.moveaxis((codes * scale).reshape(v.shape), -1, axis)


WIDE = False


def mx_kscale(k):
    if not WIDE:
        return np.ones(k)
    levels = np.array([10, -10, 5, -5, 0])
    if k % 512:
        return np.exp2(np.random.permutation(np.resize(levels, k // 32))).repeat(32)
    a = np.empty((k // 512, 16))
    for p in range(k // 512):
        a[p, :8] = np.random.permutation(np.resize(levels, 8))
        for g in range(8):
            far = levels[np.abs(levels - a[p, g]) >= 10]
            a[p, g + 8] = far[np.random.randint(len(far))]
    return np.exp2(a.ravel()).repeat(32)


def f64(x):
    return np.asarray(x).astype(np.float64)


def striped(idx):
    return np.tile(np.asarray(idx).reshape(-1, 16).T, (8, 1)).astype(np.uint16)


def unstriped(offs):
    return offs[:16].T.reshape(-1).astype(np.int64)


E2M1 = np.array([0.0, 0.5, 1.0, 1.5, 2.0, 3.0, 4.0, 6.0, -0.0, -0.5, -1.0, -1.5, -2.0, -3.0, -4.0, -6.0])


def pack_weight(w, fmt):
    k, n = w.shape
    w = f64(np.asarray(w, np.float32).astype(ml_dtypes.bfloat16)).reshape(k // 32, 32, n)
    amax = np.abs(w).max(1)
    if fmt == "e4m3":
        byte = np.frexp(amax)[1] - 1 + 127 - 7
    else:
        mant, ex = np.frexp(amax / 6.0)
        byte = np.where(mant > 0.5, ex, ex - 1) + 127
    byte = np.clip(np.where(amax > 0, byte, 1), 1, 254)
    scaled = (w * np.exp2(127.0 - byte)[:, None, :]).reshape(k, n).astype(np.float32)
    by_word = np.ascontiguousarray(scaled.reshape(k // 512, 128, 4, n).transpose(0, 1, 3, 2))
    if fmt == "e4m3":
        words = by_word.astype(ml_dtypes.float8_e4m3fn).view(np.uint8)
    else:
        c = by_word.astype(ml_dtypes.float4_e2m1fn).view(np.uint8) & 0xF
        words = (c[..., 0::2] | (c[..., 1::2] << 4)).reshape(k // 512, 128, 2 * n)
    return np.ascontiguousarray(words), np.ascontiguousarray(byte.astype(np.uint8).reshape(k // 512, 16, n))


def unpack_weight(words, scales, fmt):
    g, _, n = scales.shape
    words = np.ascontiguousarray(words).reshape(g, 128, n, -1)
    if fmt == "e4m3":
        vals = words.view(ml_dtypes.float8_e4m3fn).astype(np.float64)
    else:
        nib = np.empty((g, 128, n, 4), np.uint8)
        nib[..., 0::2] = words & 0xF
        nib[..., 1::2] = words >> 4
        vals = E2M1[nib]
    vals = vals * np.repeat(np.exp2(scales.astype(np.float64) - 127.0), 8, axis=1)[..., None]
    return vals.transpose(0, 1, 3, 2).reshape(g * 512, n)


def bf(x):
    return np.asarray(x, np.float32).astype(ml_dtypes.bfloat16)


def planes(Y):
    r, m = Y.shape
    b = f64(bf(Y)).reshape(r // 32, 32, m)
    amax = np.abs(b).max(1)
    byte = np.clip(np.where(amax > 0, np.frexp(amax)[1] - 1 + 127 - 7, 1), 1, 254)
    codes = (b * np.exp2(127.0 - byte)[:, None, :]).reshape(r, m).astype(np.float32).astype(ml_dtypes.float8_e4m3fn).view(np.uint8)
    words = codes.reshape(r // 512, 128, 4, m).transpose(0, 1, 3, 2)
    return np.ascontiguousarray(words), np.ascontiguousarray(byte.astype(np.uint8).reshape(r // 512, 16, m))


D, T, I, J, U, E, M = 512, 2048, 512, 256, 1024, 512, 1024


def setup_inputs():
    n = np.random.standard_normal
    idx = np.random.permutation(T)[:I]
    idx2 = np.random.permutation(U)[:J]
    idx3 = np.random.permutation(M)[:J]
    fd = mx_kscale(D)
    fi = mx_kscale(I)
    ti = np.ones(T)
    ti[idx] = fi
    keysp = pack_weight(n((D, T)) / fd[:, None], "e2m1")
    return {
        "keys_words": keysp[0],
        "keys_scales": keysp[1],
        "notes": (n((D, U)) * 1.0 / np.sqrt(D) * fd[:, None]).astype(np.float32),
        "rowf": (np.random.uniform(0.02, 0.08, (I, 1)) * fi[:, None]).astype(np.float32),
        "vals": (n((E, T)) / ti).astype(np.float32),
        "held": (n((E, M))).astype(np.float32),
        "hgain": np.tile(np.random.uniform(0.5, 2.0, M), (128, 1)).astype(np.float32),
        "offs": striped(idx),
        "offs2": striped(idx2),
        "offs3": striped(idx3),
    }


def reference(keys_words, keys_scales, notes, rowf, vals, held, hgain, offs, offs2, offs3):
    idx = unstriped(offs)
    idx2 = unstriped(offs2)
    idx3 = unstriped(offs3)
    keysu = unpack_weight(keys_words, keys_scales, "e2m1")
    keysidxg = keysu[:, idx]
    notesidx2q = mxq(f64(notes)[:, idx2], 0, "e4m3")
    g9 = keysidxg.T @ notesidx2q
    g0 = np.tanh(g9)
    gr1 = g0 * f64(rowf)
    vt1 = f64(vals)[:, idx].T
    vt1q = mxq(vt1, 0, "e4m3")
    gr1q = mxq(gr1, 0, "e4m3")
    o = vt1q.T @ gr1q
    y = f64(held)[:, idx3] + o * f64(hgain)[:1][:, idx3]
    words, scales = planes(y)
    return y, words, scales

@@ -1,0 +1,248 @@
+from contextlib import ExitStack
+
+import concourse.mybir as mybir
+from concourse.masks import make_identity
+
+D, T, I, J, U, E, M = 512, 2048, 512, 256, 1024, 512, 1024
+FLOPS = 2 * D * I * J + 2 * I * E * J
+
+F32 = mybir.dt.float32
+BF16 = mybir.dt.bfloat16
+I32 = mybir.dt.int32
+U32 = mybir.dt.uint32
+U16 = mybir.dt.uint16
+U8 = mybir.dt.uint8
+FP8X4 = mybir.dt.float8_e4m3fn_x4
+FP4X4 = mybir.dt.float4_e2m1fn_x4
+COPY = mybir.ActivationFunctionType.Copy
+IDENTITY = mybir.ActivationFunctionType.Identity
+TANH = mybir.ActivationFunctionType.Tanh
+MULT = mybir.AluOpType.mult
+ADD = mybir.AluOpType.add
+
+P = 128
+PACK = 4
+QUADS = 4
+HALF = J // 2
+
+
+def tile_attend_tab_plain_merge_pl_kernel(
+    tc, keys_words, keys_scales, notes, rowf, vals, held, hgain, offs, offs2, offs3, out_0, out_1, out_2
+):
+    nc = tc.nc
+    with ExitStack() as ctx:
+        lists = ctx.enter_context(tc.tile_pool(name="lists", bufs=1))
+        keep = ctx.enter_context(tc.tile_pool(name="keep", bufs=1))
+        psum1 = ctx.enter_context(tc.psum_pool(name="psum1", bufs=1))
+        psum2 = ctx.enter_context(tc.psum_pool(name="psum2", bufs=1))
+
+        tokens = lists.tile([P, I // 16], U16)
+        note_ids = lists.tile([P, J // 16], U16)
+        held_ids = lists.tile([P, J // 16], U16)
+
+        key_words = keep.tile([P, T], U16, align_bytes=64)
+        key_bytes = keep.tile([P, T], U8, align_bytes=64)
+        note_pool = [keep.tile([P, 2, U], F32, name="note_pool%d" % a) for a in range(2)]
+        row_factor = keep.tile([P, PACK], F32)
+        gain_pool = keep.tile([P, M], F32)
+        val_pool = [keep.tile([P, T], F32, name="val_pool%d" % t, tag="val_pool%d" % t) for t in range(PACK)]
+        held_pool = [keep.tile([P, M], F32, name="held_pool%d" % t) for t in range(PACK)]
+        ident = keep.tile([P, P], F32)
+
+        nc.vector.memset(key_bytes[:].bitcast(I32), 0)
+        nc.vector.memset(gain_pool[:], 0.0)
+        make_identity(nc, ident[:])
+
+        val_rows = vals.rearrange("(p t) w -> t p w", t=PACK)
+        held_rows = held.rearrange("(p t) w -> t p w", t=PACK)
+
+        staged_bytes = keep.tile([P, 2, T], U8, align_bytes=64)
+        staged_gain = keep.tile([1, M], F32)
+        nc.sync.dma_start(out=key_words[:].bitcast(I32), in_=keys_words[0].bitcast(I32))
+        for a in range(2):
+            nc.sync.dma_start(
+                out=staged_bytes[64 * a : 64 * a + 4].bitcast(I32),
+                in_=keys_scales[0, 8 * a : 8 * a + 8, :].rearrange("(b f) c -> f b c", b=2).bitcast(I32),
+            )
+        nc.sync.dma_start(tokens[:], offs)
+        nc.sync.dma_start(held_ids[:], offs3)
+        nc.sync.dma_start(out=staged_gain[:], in_=hgain[0:1, :])
+        nc.sync.dma_start(note_ids[:], offs2)
+        note_rows = notes.rearrange("(p a b) w -> a p b w", a=2, b=2)
+        for a in range(2):
+            nc.sync.dma_start(out=note_pool[a][:], in_=note_rows[a])
+        nc.sync.dma_start(out=val_pool[0][:], in_=val_rows[0])
+        nc.sync.dma_start(out=row_factor[:], in_=rowf.rearrange("(p t) o -> p (t o)", t=PACK))
+        for t in range(1, PACK):
+            nc.sync.dma_start(out=val_pool[t][:], in_=val_rows[t])
+        for t in range(PACK):
+            nc.sync.dma_start(out=held_pool[t][:], in_=held_rows[t])
+
+        for q in range(QUADS):
+            a, b = divmod(q, 2)
+            nc.vector.tensor_copy(
+                key_bytes[32 * q : 32 * q + 4, :].bitcast(I32), staged_bytes[64 * a : 64 * a + 4, b, :].bitcast(I32)
+            )
+        nc.scalar.activation(gain_pool[0:1, :], staged_gain[:], IDENTITY)
+
+        picked_words = keep.tile([P, I], U16, align_bytes=64)
+        dealt_words = keep.tile([P, PACK, P], U16, align_bytes=64)
+        dealt_bytes = keep.tile([P, PACK, P], U8, align_bytes=64)
+        nc.vector.tensor_copy(picked_words[:], key_words[:].indirect(tokens[:]))
+        nc.vector.tensor_copy(dealt_bytes[:].rearrange("p r s -> p s r"), key_bytes[:].indirect(tokens[:]))
+        nc.vector.tensor_copy(dealt_words[:], picked_words[:].rearrange("p (s r) -> p r s", r=PACK))
+
+        gain_row = keep.tile([P, J], F32)
+        nc.scalar.activation(gain_row[:], gain_pool[:].indirect(held_ids[:]), COPY)
+        gain_turned = psum1.tile([P, 2, P], F32)
+        for h in range(2):
+            nc.tensor.transpose(gain_turned[:, h, :], gain_row[:, h * P : (h + 1) * P], ident[:])
+        gain_column = keep.tile([P, 2], F32)
+        nc.scalar.copy(gain_column[:], gain_turned[:, :, 0])
+        gain_spread = psum1.tile([P, 2, P], F32)
+        for h in range(2):
+            nc.tensor.transpose(gain_spread[:, h, :], gain_column[:, h : h + 1].to_broadcast([P, P]), ident[:])
+        gain = keep.tile([P, J], F32)
+        nc.scalar.copy(gain[:], gain_spread[:].rearrange("p h j -> p (h j)"))
+
+        picked_notes = keep.tile([P, PACK, J], F32)
+        for a in range(2):
+            nc.vector.tensor_copy(picked_notes[:, 2 * a, :], note_pool[a][:, 0, :].indirect(note_ids[:]))
+            nc.scalar.activation(picked_notes[:, 2 * a + 1, :], note_pool[a][:, 1, :].indirect(note_ids[:]), COPY)
+        notes_bf = [keep.tile([P, HALF, PACK], BF16, name="notes_bf%d" % h, align_bytes=64) for h in range(2)]
+        note_codes = keep.tile([P, J], U32, align_bytes=64)
+        note_scales = keep.tile([P, J], U8, align_bytes=64)
+        for h in range(2):
+            nc.vector.tensor_copy(
+                notes_bf[h][:], picked_notes[:, :, h * HALF : (h + 1) * HALF].rearrange("p t j -> p j t")
+            )
+        for h in range(2):
+            cols = slice(h * HALF, (h + 1) * HALF)
+            nc.vector.quantize_mx(
+                out=note_codes[:, cols].bitcast(FP8X4),
+                scales=note_scales[:, cols],
+                in_=notes_bf[h][:].rearrange("p j t -> p (j t)"),
+            )
+
+        picked_vals = {}
+        result_row = keep.tile([P, PACK * J], F32, align_bytes=64)
+        result = result_row[:].rearrange("p (t j) -> p t j", t=PACK)
+        vals_bf = [keep.tile([P, P * PACK], BF16, name="vals_bf%d" % t, align_bytes=64)[:] for t in range(2)]
+        vals_bf.extend(result_row[:, t * J : (t + 1) * J].bitcast(BF16) for t in range(2))
+        val_codes = [keep.tile([P, P], U32, name="val_codes%d" % t, align_bytes=64) for t in range(PACK)]
+        val_scales = [keep.tile([P, P], U8, name="val_scales%d" % t, align_bytes=64) for t in range(PACK)]
+        table = {}
+        table_bf = keep.tile([P, J, PACK], BF16, align_bytes=64)
+        table_codes = keep.tile([P, J], U32, align_bytes=64)
+        table_scales = keep.tile([P, J], U8, align_bytes=64)
+        gained = keep.tile([P, PACK, J], F32)
+        out_rows = out_0.rearrange("(p t) j -> p t j", t=PACK)
+
+        def pick_values(t):
+            picked_vals[t] = keep.tile([P, I], BF16, name="picked_vals%d" % t, align_bytes=64)
+            nc.scalar.activation(picked_vals[t][:], val_pool[t][:].indirect(tokens[:]), COPY)
+
+        def raw_table(h):
+            cols = slice(h * HALF, (h + 1) * HALF)
+            raw = psum1.tile([P, PACK, HALF], F32, name="raw%d" % h)
+            for r in range(PACK):
+                nc.tensor.matmul_mx(
+                    out=raw[:, r, :],
+                    lhsT=dealt_words[:, r, :].bitcast(FP4X4),
+                    lhsT_scale=dealt_bytes[:, r, :],
+                    rhs=note_codes[:, cols].bitcast(FP8X4),
+                    rhs_scale=note_scales[:, cols],
+                    start=True,
+                    stop=True,
+                )
+            table[h] = keep.tile([P, HALF, PACK], F32, name="table%d" % h, tag=("val_pool0", "table1")[h])
+            nc.scalar.activation(table[h][:], raw[:].rearrange("p r j -> p j r"), TANH)
+
+        def weigh_table(h):
+            nc.vector.tensor_tensor(
+                table_bf[:, h * HALF : (h + 1) * HALF, :],
+                table[h][:],
+                row_factor[:].unsqueeze(1).to_broadcast([P, HALF, PACK]),
+                MULT,
+            )
+
+        def quantise_table():
+            nc.vector.quantize_mx(
+                out=table_codes[:].bitcast(FP8X4),
+                scales=table_scales[:],
+                in_=table_bf[:].rearrange("p j r -> p (j r)"),
+            )
+
+        def turn_values(t):
+            pairs = picked_vals[t][:].bitcast(F32)
+            turned = psum2.tile([P, 2, P], F32, name="turned%d" % t, tag="bank%d" % t)
+            for u in range(2):
+                nc.tensor.transpose(turned[:, u, :], pairs[:, u : I // 2 : 2], ident[:])
+            move = nc.scalar.copy if t == PACK - 1 else nc.vector.tensor_copy
+            move(
+                vals_bf[t].bitcast(F32).rearrange("p (m u) -> p m u", u=2), turned[:].rearrange("p u m -> p m u")
+            )
+
+        def quantise_values(t):
+            nc.vector.quantize_mx(out=val_codes[t][:].bitcast(FP8X4), scales=val_scales[t][:], in_=vals_bf[t])
+
+        def multiply(t):
+            product = psum2.tile([P, J], F32, name="product%d" % t, tag="bank%d" % (1, 2, 0, 3)[t])
+            nc.tensor.matmul_mx(
+                out=product[:],
+                lhsT=val_codes[t][:].bitcast(FP8X4),
+                lhsT_scale=val_scales[t][:],
+                rhs=table_codes[:].bitcast(FP8X4),
+                rhs_scale=table_scales[:],
+                start=True,
+                stop=True,
+            )
+            nc.vector.tensor_tensor(gained[:, t, :], product[:], gain[:], MULT)
+
+        def merge(t):
+            nc.vector.tensor_tensor(result_row[:, t * J : (t + 1) * J], held_pool[t][:].indirect(held_ids[:]), gained[:, t, :], ADD)
+
+        pick_values(0)
+        raw_table(0)
+        raw_table(1)
+        weigh_table(0)
+        pick_values(1)
+        turn_values(0)
+        weigh_table(1)
+        quantise_values(0)
+        quantise_table()
+        turn_values(1)
+        multiply(0)
+        quantise_values(1)
+        pick_values(2)
+        turn_values(2)
+        multiply(1)
+        quantise_values(2)
+        pick_values(3)
+        multiply(2)
+        merge(0)
+        turn_values(3)
+        quantise_values(3)
+        merge(1)
+        multiply(3)
+        merge(2)
+        merge(3)
+        nc.sync.dma_start(out=out_rows[:, 0 : PACK - 1, :], in_=result[:, 0 : PACK - 1, :])
+        nc.sync.dma_start(out=out_rows[:, PACK - 1, :], in_=result[:, PACK - 1, :])
+
+        result_bf = keep.tile([P, J, PACK], BF16, align_bytes=64)
+        nc.vector.tensor_copy(result_bf[:], result.rearrange("p t j -> p j t"))
+        result_codes = keep.tile([P, J], U32, align_bytes=64)
+        result_scales = keep.tile([P, J], U8, align_bytes=64)
+        nc.vector.quantize_mx(
+            out=result_codes[:].bitcast(FP8X4), scales=result_scales[:], in_=result_bf[:].rearrange("p j t -> p (j t)")
+        )
+        nc.sync.dma_start(
+            out=out_1[0].rearrange("p c r -> p (c r)").bitcast(I32), in_=result_codes[:].bitcast(I32)
+        )
+        for q in range(QUADS):
+            queue = nc.scalar if q % 2 == 0 else nc.sync
+            queue.dma_start(
+                out=out_2[0, 4 * q : 4 * q + 4, :].bitcast(I32),
+                in_=result_scales[32 * q : 32 * q + 4, :].bitcast(I32),
+            )

@@ -15,7 +15,6 @@ U8 = mybir.dt.uint8
 FP8X4 = mybir.dt.float8_e4m3fn_x4
 FP4X4 = mybir.dt.float4_e2m1fn_x4
 COPY = mybir.ActivationFunctionType.Copy
-IDENTITY = mybir.ActivationFunctionType.Identity
 TANH = mybir.ActivationFunctionType.Tanh
 MULT = mybir.AluOpType.mult
 ADD = mybir.AluOpType.add
@@ -45,7 +44,7 @@ def tile_attend_tab_plain_merge_pl_kernel(
         note_pool = [keep.tile([P, 2, U], F32, name="note_pool%d" % a) for a in range(2)]
         row_factor = keep.tile([P, PACK], F32)
         gain_pool = keep.tile([P, M], F32)
-        val_pool = [keep.tile([P, T], F32, name="val_pool%d" % t, tag="val_pool%d" % t) for t in range(PACK)]
+        val_pool = [keep.tile([P, T], F32, name="val_pool%d" % t, tag="val_pool%d" % t, align_bytes=64) for t in range(PACK)]
         held_pool = [keep.tile([P, M], F32, name="held_pool%d" % t) for t in range(PACK)]
         ident = keep.tile([P, P], F32)
 
@@ -56,34 +55,25 @@ def tile_attend_tab_plain_merge_pl_kernel(
         val_rows = vals.rearrange("(p t) w -> t p w", t=PACK)
         held_rows = held.rearrange("(p t) w -> t p w", t=PACK)
 
-        staged_bytes = keep.tile([P, 2, T], U8, align_bytes=64)
-        staged_gain = keep.tile([1, M], F32)
+        note_rows = notes.rearrange("(p a b) w -> a p b w", a=2, b=2)
         nc.sync.dma_start(out=key_words[:].bitcast(I32), in_=keys_words[0].bitcast(I32))
-        for a in range(2):
+        for q in range(QUADS):
             nc.sync.dma_start(
-                out=staged_bytes[64 * a : 64 * a + 4].bitcast(I32),
-                in_=keys_scales[0, 8 * a : 8 * a + 8, :].rearrange("(b f) c -> f b c", b=2).bitcast(I32),
+                out=key_bytes[32 * q : 32 * q + 4, :].bitcast(I32),
+                in_=keys_scales[0, 4 * q : 4 * q + 4, :].bitcast(I32),
             )
         nc.sync.dma_start(tokens[:], offs)
-        nc.sync.dma_start(held_ids[:], offs3)
-        nc.sync.dma_start(out=staged_gain[:], in_=hgain[0:1, :])
         nc.sync.dma_start(note_ids[:], offs2)
-        note_rows = notes.rearrange("(p a b) w -> a p b w", a=2, b=2)
         for a in range(2):
             nc.sync.dma_start(out=note_pool[a][:], in_=note_rows[a])
+        nc.sync.dma_start(out=gain_pool[0:1, :], in_=hgain[0:1, :])
+        nc.sync.dma_start(held_ids[:], offs3)
         nc.sync.dma_start(out=val_pool[0][:], in_=val_rows[0])
         nc.sync.dma_start(out=row_factor[:], in_=rowf.rearrange("(p t) o -> p (t o)", t=PACK))
         for t in range(1, PACK):
             nc.sync.dma_start(out=val_pool[t][:], in_=val_rows[t])
         for t in range(PACK):
             nc.sync.dma_start(out=held_pool[t][:], in_=held_rows[t])
-
-        for q in range(QUADS):
-            a, b = divmod(q, 2)
-            nc.vector.tensor_copy(
-                key_bytes[32 * q : 32 * q + 4, :].bitcast(I32), staged_bytes[64 * a : 64 * a + 4, b, :].bitcast(I32)
-            )
-        nc.scalar.activation(gain_pool[0:1, :], staged_gain[:], IDENTITY)
 
         picked_words = keep.tile([P, I], U16, align_bytes=64)
         dealt_words = keep.tile([P, PACK, P], U16, align_bytes=64)
@@ -98,12 +88,7 @@ def tile_attend_tab_plain_merge_pl_kernel(
         for h in range(2):
             nc.tensor.transpose(gain_turned[:, h, :], gain_row[:, h * P : (h + 1) * P], ident[:])
         gain_column = keep.tile([P, 2], F32)
-        nc.scalar.copy(gain_column[:], gain_turned[:, :, 0])
-        gain_spread = psum1.tile([P, 2, P], F32)
-        for h in range(2):
-            nc.tensor.transpose(gain_spread[:, h, :], gain_column[:, h : h + 1].to_broadcast([P, P]), ident[:])
-        gain = keep.tile([P, J], F32)
-        nc.scalar.copy(gain[:], gain_spread[:].rearrange("p h j -> p (h j)"))
+        nc.vector.tensor_copy(gain_column[:], gain_turned[:, :, 0])
 
         picked_notes = keep.tile([P, PACK, J], F32)
         for a in range(2):
@@ -125,17 +110,18 @@ def tile_attend_tab_plain_merge_pl_kernel(
             )
 
         picked_vals = {}
-        result_row = keep.tile([P, PACK * J], F32, align_bytes=64)
-        result = result_row[:].rearrange("p (t j) -> p t j", t=PACK)
-        vals_bf = [keep.tile([P, P * PACK], BF16, name="vals_bf%d" % t, align_bytes=64)[:] for t in range(2)]
-        vals_bf.extend(result_row[:, t * J : (t + 1) * J].bitcast(BF16) for t in range(2))
-        val_codes = [keep.tile([P, P], U32, name="val_codes%d" % t, align_bytes=64) for t in range(PACK)]
+        result = keep.tile([P, PACK, J], F32)
+        vals_bf = [keep.tile([P, P * PACK], BF16, name="vals_bf%d" % t, tag="vals_bf%d" % t, align_bytes=64)[:] for t in range(PACK)]
+        val_codes = {}
         val_scales = [keep.tile([P, P], U8, name="val_scales%d" % t, align_bytes=64) for t in range(PACK)]
         table = {}
         table_bf = keep.tile([P, J, PACK], BF16, align_bytes=64)
         table_codes = keep.tile([P, J], U32, align_bytes=64)
         table_scales = keep.tile([P, J], U8, align_bytes=64)
-        gained = keep.tile([P, PACK, J], F32)
+        gained = {}
+        product = {}
+        picked_held = {}
+        gain = keep.tile([P, J], F32)
         out_rows = out_0.rearrange("(p t) j -> p t j", t=PACK)
 
         def pick_values(t):
@@ -144,7 +130,7 @@ def tile_attend_tab_plain_merge_pl_kernel(
 
         def raw_table(h):
             cols = slice(h * HALF, (h + 1) * HALF)
-            raw = psum1.tile([P, PACK, HALF], F32, name="raw%d" % h)
+            raw = psum1.tile([P, PACK, HALF], F32, name="raw%d" % h, tag="raw%d" % h)
             for r in range(PACK):
                 nc.tensor.matmul_mx(
                     out=raw[:, r, :],
@@ -155,8 +141,14 @@ def tile_attend_tab_plain_merge_pl_kernel(
                     start=True,
                     stop=True,
                 )
-            table[h] = keep.tile([P, HALF, PACK], F32, name="table%d" % h, tag=("val_pool0", "table1")[h])
+            table[h] = keep.tile([P, HALF, PACK], F32, name="table%d" % h, tag=("val_pool0", "table1")[h], align_bytes=64)
             nc.scalar.activation(table[h][:], raw[:].rearrange("p r j -> p j r"), TANH)
+
+        def spread_gain():
+            gain_spread = psum1.tile([P, 2, P], F32, tag="raw0")
+            for h in range(2):
+                nc.tensor.transpose(gain_spread[:, h, :], gain_column[:, h : h + 1].to_broadcast([P, P]), ident[:])
+            nc.vector.tensor_copy(gain[:], gain_spread[:].rearrange("p h j -> p (h j)"))
 
         def weigh_table(h):
             nc.vector.tensor_tensor(
@@ -178,18 +170,18 @@ def tile_attend_tab_plain_merge_pl_kernel(
             turned = psum2.tile([P, 2, P], F32, name="turned%d" % t, tag="bank%d" % t)
             for u in range(2):
                 nc.tensor.transpose(turned[:, u, :], pairs[:, u : I // 2 : 2], ident[:])
-            move = nc.scalar.copy if t == PACK - 1 else nc.vector.tensor_copy
-            move(
+            nc.vector.tensor_copy(
                 vals_bf[t].bitcast(F32).rearrange("p (m u) -> p m u", u=2), turned[:].rearrange("p u m -> p m u")
             )
 
         def quantise_values(t):
+            val_codes[t] = keep.tile([P, P], U32, name="val_codes%d" % t, tag="val_pool%d" % (t + 1), align_bytes=64)
             nc.vector.quantize_mx(out=val_codes[t][:].bitcast(FP8X4), scales=val_scales[t][:], in_=vals_bf[t])
 
         def multiply(t):
-            product = psum2.tile([P, J], F32, name="product%d" % t, tag="bank%d" % (1, 2, 0, 3)[t])
+            product[t] = psum2.tile([P, J], F32, name="product%d" % t, tag="bank%d" % t)
             nc.tensor.matmul_mx(
-                out=product[:],
+                out=product[t][:],
                 lhsT=val_codes[t][:].bitcast(FP8X4),
                 lhsT_scale=val_scales[t][:],
                 rhs=table_codes[:].bitcast(FP8X4),
@@ -197,10 +189,18 @@ def tile_attend_tab_plain_merge_pl_kernel(
                 start=True,
                 stop=True,
             )
-            nc.vector.tensor_tensor(gained[:, t, :], product[:], gain[:], MULT)
+
+        def apply_gain(t):
+            tag = "vals_bf3" if t == 2 else "gained%d" % t
+            gained[t] = keep.tile([P, J], F32, name="gained%d" % t, tag=tag, align_bytes=64)
+            nc.vector.tensor_tensor(gained[t][:], product[t][:], gain[:], MULT)
+
+        def pick_held(t):
+            picked_held[t] = keep.tile([P, J], F32, name="picked_held%d" % t)
+            nc.scalar.activation(picked_held[t][:], held_pool[t][:].indirect(held_ids[:]), COPY)
 
         def merge(t):
-            nc.vector.tensor_tensor(result_row[:, t * J : (t + 1) * J], held_pool[t][:].indirect(held_ids[:]), gained[:, t, :], ADD)
+            nc.vector.tensor_tensor(result[:, t, :], picked_held[t][:], gained[t][:], ADD)
 
         pick_values(0)
         raw_table(0)
@@ -208,35 +208,44 @@ def tile_attend_tab_plain_merge_pl_kernel(
         weigh_table(0)
         pick_values(1)
         turn_values(0)
+        spread_gain()
         weigh_table(1)
-        quantise_values(0)
         quantise_table()
-        turn_values(1)
-        multiply(0)
-        quantise_values(1)
         pick_values(2)
-        turn_values(2)
-        multiply(1)
-        quantise_values(2)
+        turn_values(1)
+        quantise_values(0)
+        multiply(0)
+        apply_gain(0)
         pick_values(3)
-        multiply(2)
-        merge(0)
+        turn_values(2)
+        quantise_values(1)
+        multiply(1)
+        apply_gain(1)
         turn_values(3)
+        quantise_values(2)
+        multiply(2)
         quantise_values(3)
-        merge(1)
+        apply_gain(2)
         multiply(3)
-        merge(2)
-        merge(3)
+        apply_gain(3)
+        for t in range(PACK):
+            pick_held(t)
+            merge(t)
         nc.sync.dma_start(out=out_rows[:, 0 : PACK - 1, :], in_=result[:, 0 : PACK - 1, :])
         nc.sync.dma_start(out=out_rows[:, PACK - 1, :], in_=result[:, PACK - 1, :])
 
-        result_bf = keep.tile([P, J, PACK], BF16, align_bytes=64)
-        nc.vector.tensor_copy(result_bf[:], result.rearrange("p t j -> p j t"))
+        result_bf = [keep.tile([P, HALF, PACK], BF16, name="result_bf%d" % h, align_bytes=64) for h in range(2)]
         result_codes = keep.tile([P, J], U32, align_bytes=64)
         result_scales = keep.tile([P, J], U8, align_bytes=64)
-        nc.vector.quantize_mx(
-            out=result_codes[:].bitcast(FP8X4), scales=result_scales[:], in_=result_bf[:].rearrange("p j t -> p (j t)")
-        )
+        for h, move in enumerate((nc.vector.tensor_copy, nc.scalar.copy)):
+            move(result_bf[h][:], result[:, :, h * HALF : (h + 1) * HALF].rearrange("p t j -> p j t"))
+        for h in range(2):
+            cols = slice(h * HALF, (h + 1) * HALF)
+            nc.vector.quantize_mx(
+                out=result_codes[:, cols].bitcast(FP8X4),
+                scales=result_scales[:, cols],
+                in_=result_bf[h][:].rearrange("p j t -> p (j t)"),
+            )
         nc.sync.dma_start(
             out=out_1[0].rearrange("p c r -> p (c r)").bitcast(I32), in_=result_codes[:].bitcast(I32)
         )

@@ -45,7 +45,9 @@ def tile_attend_tab_plain_merge_pl_kernel(
         row_factor = keep.tile([P, PACK], F32)
         gain_pool = keep.tile([P, M], F32)
         val_pool = [keep.tile([P, T], F32, name="val_pool%d" % t, tag="val_pool%d" % t, align_bytes=64) for t in range(PACK)]
-        held_pool = [keep.tile([P, M], F32, name="held_pool%d" % t) for t in range(PACK)]
+        held_pair = keep.tile([P, 2, M], F32)
+        held_pool = [held_pair[:, 0, :], held_pair[:, 1, :]]
+        held_pool.extend(keep.tile([P, M], F32, name="held_pool%d" % t)[:] for t in range(2, PACK))
         ident = keep.tile([P, P], F32)
 
         nc.vector.memset(key_bytes[:].bitcast(I32), 0)
@@ -57,10 +59,10 @@ def tile_attend_tab_plain_merge_pl_kernel(
 
         note_rows = notes.rearrange("(p a b) w -> a p b w", a=2, b=2)
         nc.sync.dma_start(out=key_words[:].bitcast(I32), in_=keys_words[0].bitcast(I32))
-        for q in range(QUADS):
+        for f in range(4):
             nc.sync.dma_start(
-                out=key_bytes[32 * q : 32 * q + 4, :].bitcast(I32),
-                in_=keys_scales[0, 4 * q : 4 * q + 4, :].bitcast(I32),
+                out=key_bytes[f:P:32, :].bitcast(I32),
+                in_=keys_scales[0, f:16:4, :].bitcast(I32),
             )
         nc.sync.dma_start(tokens[:], offs)
         nc.sync.dma_start(note_ids[:], offs2)
@@ -72,8 +74,9 @@ def tile_attend_tab_plain_merge_pl_kernel(
         nc.sync.dma_start(out=row_factor[:], in_=rowf.rearrange("(p t) o -> p (t o)", t=PACK))
         for t in range(1, PACK):
             nc.sync.dma_start(out=val_pool[t][:], in_=val_rows[t])
-        for t in range(PACK):
-            nc.sync.dma_start(out=held_pool[t][:], in_=held_rows[t])
+        nc.sync.dma_start(out=held_pair[:], in_=held.rearrange("(p t) w -> p t w", t=PACK)[:, 0:2, :])
+        for t in range(2, PACK):
+            nc.sync.dma_start(out=held_pool[t], in_=held_rows[t])
 
         picked_words = keep.tile([P, I], U16, align_bytes=64)
         dealt_words = keep.tile([P, PACK, P], U16, align_bytes=64)
@@ -111,7 +114,7 @@ def tile_attend_tab_plain_merge_pl_kernel(
 
         picked_vals = {}
         result = keep.tile([P, PACK, J], F32)
-        vals_bf = [keep.tile([P, P * PACK], BF16, name="vals_bf%d" % t, tag="vals_bf%d" % t, align_bytes=64)[:] for t in range(PACK)]
+        vals_bf = {}
         val_codes = {}
         val_scales = [keep.tile([P, P], U8, name="val_scales%d" % t, align_bytes=64) for t in range(PACK)]
         table = {}
@@ -126,7 +129,11 @@ def tile_attend_tab_plain_merge_pl_kernel(
 
         def pick_values(t):
             picked_vals[t] = keep.tile([P, I], BF16, name="picked_vals%d" % t, align_bytes=64)
-            nc.scalar.activation(picked_vals[t][:], val_pool[t][:].indirect(tokens[:]), COPY)
+            if t < PACK - 1:
+                nc.scalar.activation(picked_vals[t][:], val_pool[t][:].indirect(tokens[:]), COPY)
+            else:
+                nc.scalar.activation(picked_vals[t][:, : I // 2], val_pool[t][:].indirect(tokens[:, : I // 32]), COPY)
+                nc.vector.tensor_copy(picked_vals[t][:, I // 2 :], val_pool[t][:].indirect(tokens[:, I // 32 :]))
 
         def raw_table(h):
             cols = slice(h * HALF, (h + 1) * HALF)
@@ -170,12 +177,15 @@ def tile_attend_tab_plain_merge_pl_kernel(
             turned = psum2.tile([P, 2, P], F32, name="turned%d" % t, tag="bank%d" % t)
             for u in range(2):
                 nc.tensor.transpose(turned[:, u, :], pairs[:, u : I // 2 : 2], ident[:])
+            tag = "val_pool3" if t == 2 else "vals_bf%d" % t
+            vals_bf[t] = keep.tile([P, P * PACK], BF16, name="vals_bf%d" % t, tag=tag, align_bytes=64)[:]
             nc.vector.tensor_copy(
                 vals_bf[t].bitcast(F32).rearrange("p (m u) -> p m u", u=2), turned[:].rearrange("p u m -> p m u")
             )
 
         def quantise_values(t):
-            val_codes[t] = keep.tile([P, P], U32, name="val_codes%d" % t, tag="val_pool%d" % (t + 1), align_bytes=64)
+            tag = "val_pool%d" % (t + 1) if t < 2 else "val_codes%d" % t
+            val_codes[t] = keep.tile([P, P], U32, name="val_codes%d" % t, tag=tag, align_bytes=64)
             nc.vector.quantize_mx(out=val_codes[t][:].bitcast(FP8X4), scales=val_scales[t][:], in_=vals_bf[t])
 
         def multiply(t):
@@ -191,13 +201,13 @@ def tile_attend_tab_plain_merge_pl_kernel(
             )
 
         def apply_gain(t):
-            tag = "vals_bf3" if t == 2 else "gained%d" % t
+            tag = ("gained0", "val_pool3", "vals_bf3", "gained3")[t]
             gained[t] = keep.tile([P, J], F32, name="gained%d" % t, tag=tag, align_bytes=64)
             nc.vector.tensor_tensor(gained[t][:], product[t][:], gain[:], MULT)
 
         def pick_held(t):
             picked_held[t] = keep.tile([P, J], F32, name="picked_held%d" % t)
-            nc.scalar.activation(picked_held[t][:], held_pool[t][:].indirect(held_ids[:]), COPY)
+            nc.scalar.activation(picked_held[t][:], held_pool[t].indirect(held_ids[:]), COPY)
 
         def merge(t):
             nc.vector.tensor_tensor(result[:, t, :], picked_held[t][:], gained[t][:], ADD)
@@ -220,26 +230,33 @@ def tile_attend_tab_plain_merge_pl_kernel(
         turn_values(2)
         quantise_values(1)
         multiply(1)
-        apply_gain(1)
         turn_values(3)
         quantise_values(2)
+        apply_gain(1)
         multiply(2)
         quantise_values(3)
         apply_gain(2)
         multiply(3)
         apply_gain(3)
-        for t in range(PACK):
+        for t in range(PACK - 1):
             pick_held(t)
             merge(t)
+        last = PACK - 1
+        last_held = keep.tile([P, HALF], F32)
+        nc.scalar.activation(last_held[:], held_pool[last].indirect(held_ids[:, HALF // 16 :]), COPY)
+        nc.vector.tensor_tensor(
+            result[:, last, :HALF], held_pool[last].indirect(held_ids[:, : HALF // 16]), gained[last][:, :HALF], ADD
+        )
+        nc.vector.tensor_tensor(result[:, last, HALF:], last_held[:], gained[last][:, HALF:], ADD)
         nc.sync.dma_start(out=out_rows[:, 0 : PACK - 1, :], in_=result[:, 0 : PACK - 1, :])
         nc.sync.dma_start(out=out_rows[:, PACK - 1, :], in_=result[:, PACK - 1, :])
 
         result_bf = [keep.tile([P, HALF, PACK], BF16, name="result_bf%d" % h, align_bytes=64) for h in range(2)]
         result_codes = keep.tile([P, J], U32, align_bytes=64)
         result_scales = keep.tile([P, J], U8, align_bytes=64)
-        for h, move in enumerate((nc.vector.tensor_copy, nc.scalar.copy)):
+        for h, move in enumerate((nc.scalar.copy, nc.vector.tensor_copy)):
             move(result_bf[h][:], result[:, :, h * HALF : (h + 1) * HALF].rearrange("p t j -> p j t"))
-        for h in range(2):
+        for h in (1, 0):
             cols = slice(h * HALF, (h + 1) * HALF)
             nc.vector.quantize_mx(
                 out=result_codes[:, cols].bitcast(FP8X4),

from contextlib import ExitStack

import concourse.mybir as mybir
from concourse.masks import make_identity

D, T, I, J, U, E, M = 512, 2048, 512, 256, 1024, 512, 1024
FLOPS = 2 * D * I * J + 2 * I * E * J

F32 = mybir.dt.float32
BF16 = mybir.dt.bfloat16
I32 = mybir.dt.int32
U32 = mybir.dt.uint32
U16 = mybir.dt.uint16
U8 = mybir.dt.uint8
FP8X4 = mybir.dt.float8_e4m3fn_x4
FP4X4 = mybir.dt.float4_e2m1fn_x4
COPY = mybir.ActivationFunctionType.Copy
TANH = mybir.ActivationFunctionType.Tanh
MULT = mybir.AluOpType.mult
ADD = mybir.AluOpType.add

P = 128
PACK = 4
QUADS = 4
HALF = J // 2


def tile_attend_tab_plain_merge_pl_kernel(
    tc, keys_words, keys_scales, notes, rowf, vals, held, hgain, offs, offs2, offs3, out_0, out_1, out_2
):
    nc = tc.nc
    with ExitStack() as ctx:
        lists = ctx.enter_context(tc.tile_pool(name="lists", bufs=1))
        keep = ctx.enter_context(tc.tile_pool(name="keep", bufs=1))
        psum1 = ctx.enter_context(tc.psum_pool(name="psum1", bufs=1))
        psum2 = ctx.enter_context(tc.psum_pool(name="psum2", bufs=1))

        tokens = lists.tile([P, I // 16], U16)
        note_ids = lists.tile([P, J // 16], U16)
        held_ids = lists.tile([P, J // 16], U16)

        key_words = keep.tile([P, T], U16, align_bytes=64)
        key_bytes = keep.tile([P, T], U8, align_bytes=64)
        note_pool = [keep.tile([P, 2, U], F32, name="note_pool%d" % a) for a in range(2)]
        row_factor = keep.tile([P, PACK], F32)
        gain_pool = keep.tile([P, M], F32)
        val_pool = [keep.tile([P, T], F32, name="val_pool%d" % t, tag="val_pool%d" % t, align_bytes=64) for t in range(PACK)]
        held_pair = keep.tile([P, 2, M], F32)
        held_pool = [held_pair[:, 0, :], held_pair[:, 1, :]]
        held_pool.extend(keep.tile([P, M], F32, name="held_pool%d" % t)[:] for t in range(2, PACK))
        ident = keep.tile([P, P], F32)

        nc.vector.memset(key_bytes[:].bitcast(I32), 0)
        nc.vector.memset(gain_pool[:], 0.0)
        make_identity(nc, ident[:])

        val_rows = vals.rearrange("(p t) w -> t p w", t=PACK)
        held_rows = held.rearrange("(p t) w -> t p w", t=PACK)

        note_rows = notes.rearrange("(p a b) w -> a p b w", a=2, b=2)
        nc.sync.dma_start(out=key_words[:].bitcast(I32), in_=keys_words[0].bitcast(I32))
        for f in range(4):
            nc.sync.dma_start(
                out=key_bytes[f:P:32, :].bitcast(I32),
                in_=keys_scales[0, f:16:4, :].bitcast(I32),
            )
        nc.sync.dma_start(tokens[:], offs)
        nc.sync.dma_start(note_ids[:], offs2)
        for a in range(2):
            nc.sync.dma_start(out=note_pool[a][:], in_=note_rows[a])
        nc.sync.dma_start(out=gain_pool[0:1, :], in_=hgain[0:1, :])
        nc.sync.dma_start(held_ids[:], offs3)
        nc.sync.dma_start(out=val_pool[0][:], in_=val_rows[0])
        nc.sync.dma_start(out=row_factor[:], in_=rowf.rearrange("(p t) o -> p (t o)", t=PACK))
        for t in range(1, PACK):
            nc.sync.dma_start(out=val_pool[t][:], in_=val_rows[t])
        nc.sync.dma_start(out=held_pair[:], in_=held.rearrange("(p t) w -> p t w", t=PACK)[:, 0:2, :])
        for t in range(2, PACK):
            nc.sync.dma_start(out=held_pool[t], in_=held_rows[t])

        picked_words = keep.tile([P, I], U16, align_bytes=64)
        dealt_words = keep.tile([P, PACK, P], U16, align_bytes=64)
        dealt_bytes = keep.tile([P, PACK, P], U8, align_bytes=64)
        nc.vector.tensor_copy(picked_words[:], key_words[:].indirect(tokens[:]))
        nc.vector.tensor_copy(dealt_bytes[:].rearrange("p r s -> p s r"), key_bytes[:].indirect(tokens[:]))
        nc.vector.tensor_copy(dealt_words[:], picked_words[:].rearrange("p (s r) -> p r s", r=PACK))

        gain_row = keep.tile([P, J], F32)
        nc.scalar.activation(gain_row[:], gain_pool[:].indirect(held_ids[:]), COPY)
        gain_turned = psum1.tile([P, 2, P], F32)
        for h in range(2):
            nc.tensor.transpose(gain_turned[:, h, :], gain_row[:, h * P : (h + 1) * P], ident[:])
        gain_column = keep.tile([P, 2], F32)
        nc.vector.tensor_copy(gain_column[:], gain_turned[:, :, 0])

        picked_notes = keep.tile([P, PACK, J], F32)
        for a in range(2):
            nc.vector.tensor_copy(picked_notes[:, 2 * a, :], note_pool[a][:, 0, :].indirect(note_ids[:]))
            nc.scalar.activation(picked_notes[:, 2 * a + 1, :], note_pool[a][:, 1, :].indirect(note_ids[:]), COPY)
        notes_bf = [keep.tile([P, HALF, PACK], BF16, name="notes_bf%d" % h, align_bytes=64) for h in range(2)]
        note_codes = keep.tile([P, J], U32, align_bytes=64)
        note_scales = keep.tile([P, J], U8, align_bytes=64)
        for h in range(2):
            nc.vector.tensor_copy(
                notes_bf[h][:], picked_notes[:, :, h * HALF : (h + 1) * HALF].rearrange("p t j -> p j t")
            )
        for h in range(2):
            cols = slice(h * HALF, (h + 1) * HALF)
            nc.vector.quantize_mx(
                out=note_codes[:, cols].bitcast(FP8X4),
                scales=note_scales[:, cols],
                in_=notes_bf[h][:].rearrange("p j t -> p (j t)"),
            )

        picked_vals = {}
        result = keep.tile([P, PACK, J], F32)
        vals_bf = {}
        val_codes = {}
        val_scales = [keep.tile([P, P], U8, name="val_scales%d" % t, align_bytes=64) for t in range(PACK)]
        table = {}
        table_bf = keep.tile([P, J, PACK], BF16, align_bytes=64)
        table_codes = keep.tile([P, J], U32, align_bytes=64)
        table_scales = keep.tile([P, J], U8, align_bytes=64)
        gained = {}
        product = {}
        picked_held = {}
        gain = keep.tile([P, J], F32)
        out_rows = out_0.rearrange("(p t) j -> p t j", t=PACK)

        def pick_values(t):
            picked_vals[t] = keep.tile([P, I], BF16, name="picked_vals%d" % t, align_bytes=64)
            if t < PACK - 1:
                nc.scalar.activation(picked_vals[t][:], val_pool[t][:].indirect(tokens[:]), COPY)
            else:
                nc.scalar.activation(picked_vals[t][:, : I // 2], val_pool[t][:].indirect(tokens[:, : I // 32]), COPY)
                nc.vector.tensor_copy(picked_vals[t][:, I // 2 :], val_pool[t][:].indirect(tokens[:, I // 32 :]))

        def raw_table(h):
            cols = slice(h * HALF, (h + 1) * HALF)
            raw = psum1.tile([P, PACK, HALF], F32, name="raw%d" % h, tag="raw%d" % h)
            for r in range(PACK):
                nc.tensor.matmul_mx(
                    out=raw[:, r, :],
                    lhsT=dealt_words[:, r, :].bitcast(FP4X4),
                    lhsT_scale=dealt_bytes[:, r, :],
                    rhs=note_codes[:, cols].bitcast(FP8X4),
                    rhs_scale=note_scales[:, cols],
                    start=True,
                    stop=True,
                )
            table[h] = keep.tile([P, HALF, PACK], F32, name="table%d" % h, tag=("val_pool0", "table1")[h], align_bytes=64)
            nc.scalar.activation(table[h][:], raw[:].rearrange("p r j -> p j r"), TANH)

        def spread_gain():
            gain_spread = psum1.tile([P, 2, P], F32, tag="raw0")
            for h in range(2):
                nc.tensor.transpose(gain_spread[:, h, :], gain_column[:, h : h + 1].to_broadcast([P, P]), ident[:])
            nc.vector.tensor_copy(gain[:], gain_spread[:].rearrange("p h j -> p (h j)"))

        def weigh_table(h):
            nc.vector.tensor_tensor(
                table_bf[:, h * HALF : (h + 1) * HALF, :],
                table[h][:],
                row_factor[:].unsqueeze(1).to_broadcast([P, HALF, PACK]),
                MULT,
            )

        def quantise_table():
            nc.vector.quantize_mx(
                out=table_codes[:].bitcast(FP8X4),
                scales=table_scales[:],
                in_=table_bf[:].rearrange("p j r -> p (j r)"),
            )

        def turn_values(t):
            pairs = picked_vals[t][:].bitcast(F32)
            turned = psum2.tile([P, 2, P], F32, name="turned%d" % t, tag="bank%d" % t)
            for u in range(2):
                nc.tensor.transpose(turned[:, u, :], pairs[:, u : I // 2 : 2], ident[:])
            tag = "val_pool3" if t == 2 else "vals_bf%d" % t
            vals_bf[t] = keep.tile([P, P * PACK], BF16, name="vals_bf%d" % t, tag=tag, align_bytes=64)[:]
            nc.vector.tensor_copy(
                vals_bf[t].bitcast(F32).rearrange("p (m u) -> p m u", u=2), turned[:].rearrange("p u m -> p m u")
            )

        def quantise_values(t):
            tag = "val_pool%d" % (t + 1) if t < 2 else "val_codes%d" % t
            val_codes[t] = keep.tile([P, P], U32, name="val_codes%d" % t, tag=tag, align_bytes=64)
            nc.vector.quantize_mx(out=val_codes[t][:].bitcast(FP8X4), scales=val_scales[t][:], in_=vals_bf[t])

        def multiply(t):
            product[t] = psum2.tile([P, J], F32, name="product%d" % t, tag="bank%d" % t)
            nc.tensor.matmul_mx(
                out=product[t][:],
                lhsT=val_codes[t][:].bitcast(FP8X4),
                lhsT_scale=val_scales[t][:],
                rhs=table_codes[:].bitcast(FP8X4),
                rhs_scale=table_scales[:],
                start=True,
                stop=True,
            )

        def apply_gain(t):
            tag = ("gained0", "val_pool3", "vals_bf3", "gained3")[t]
            gained[t] = keep.tile([P, J], F32, name="gained%d" % t, tag=tag, align_bytes=64)
            nc.vector.tensor_tensor(gained[t][:], product[t][:], gain[:], MULT)

        def pick_held(t):
            picked_held[t] = keep.tile([P, J], F32, name="picked_held%d" % t)
            nc.scalar.activation(picked_held[t][:], held_pool[t].indirect(held_ids[:]), COPY)

        def merge(t):
            nc.vector.tensor_tensor(result[:, t, :], picked_held[t][:], gained[t][:], ADD)

        pick_values(0)
        raw_table(0)
        raw_table(1)
        weigh_table(0)
        pick_values(1)
        turn_values(0)
        spread_gain()
        weigh_table(1)
        quantise_table()
        pick_values(2)
        turn_values(1)
        quantise_values(0)
        multiply(0)
        apply_gain(0)
        pick_values(3)
        turn_values(2)
        quantise_values(1)
        multiply(1)
        turn_values(3)
        quantise_values(2)
        apply_gain(1)
        multiply(2)
        quantise_values(3)
        apply_gain(2)
        multiply(3)
        apply_gain(3)
        for t in range(PACK - 1):
            pick_held(t)
            merge(t)
        last = PACK - 1
        last_held = keep.tile([P, HALF], F32)
        nc.scalar.activation(last_held[:], held_pool[last].indirect(held_ids[:, HALF // 16 :]), COPY)
        nc.vector.tensor_tensor(
            result[:, last, :HALF], held_pool[last].indirect(held_ids[:, : HALF // 16]), gained[last][:, :HALF], ADD
        )
        nc.vector.tensor_tensor(result[:, last, HALF:], last_held[:], gained[last][:, HALF:], ADD)
        nc.sync.dma_start(out=out_rows[:, 0 : PACK - 1, :], in_=result[:, 0 : PACK - 1, :])
        nc.sync.dma_start(out=out_rows[:, PACK - 1, :], in_=result[:, PACK - 1, :])

        result_bf = [keep.tile([P, HALF, PACK], BF16, name="result_bf%d" % h, align_bytes=64) for h in range(2)]
        result_codes = keep.tile([P, J], U32, align_bytes=64)
        result_scales = keep.tile([P, J], U8, align_bytes=64)
        for h, move in enumerate((nc.scalar.copy, nc.vector.tensor_copy)):
            move(result_bf[h][:], result[:, :, h * HALF : (h + 1) * HALF].rearrange("p t j -> p j t"))
        for h in (1, 0):
            cols = slice(h * HALF, (h + 1) * HALF)
            nc.vector.quantize_mx(
                out=result_codes[:, cols].bitcast(FP8X4),
                scales=result_scales[:, cols],
                in_=result_bf[h][:].rearrange("p j t -> p (j t)"),
            )
        nc.sync.dma_start(
            out=out_1[0].rearrange("p c r -> p (c r)").bitcast(I32), in_=result_codes[:].bitcast(I32)
        )
        for q in range(QUADS):
            queue = nc.scalar if q % 2 == 0 else nc.sync
            queue.dma_start(
                out=out_2[0, 4 * q : 4 * q + 4, :].bitcast(I32),
                in_=result_scales[32 * q : 32 * q + 4, :].bitcast(I32),
            )
